import numpy as np
import ml_dtypes


def mxq(x, axis, fmt="e4m3"):
    dtype, down = {"e4m3": (ml_dtypes.float8_e4m3fn, 7), "e5m2": (ml_dtypes.float8_e5m2, 14)}[fmt]
    v = np.moveaxis(np.asarray(x, np.float32).astype(ml_dtypes.bfloat16).astype(np.float64), axis, -1)
    blocks = v.reshape(v.shape[:-1] + (-1, 32))
    amax = np.abs(blocks).max(-1, keepdims=True)
    byte = np.maximum(np.where(amax > 0, np.frexp(amax)[1] - 1 + 127, 0) - down, 1)
    scale = np.exp2(byte - 127.0)
    codes = (blocks / scale).astype(np.float32).astype(dtype).astype(np.float64)
    return np.moveaxis((codes * scale).reshape(v.shape), -1, axis)


WIDE = False


def mx_kscale(k):
    if not WIDE:
        return np.ones(k)
    levels = np.array([10, -10, 5, -5, 0])
    if k % 512:
        return np.exp2(np.random.permutation(np.resize(levels, k // 32))).repeat(32)
    a = np.empty((k // 512, 16))
    for p in range(k // 512):
        a[p, :8] = np.random.permutation(np.resize(levels, 8))
        for g in range(8):
            far = levels[np.abs(levels - a[p, g]) >= 10]
            a[p, g + 8] = far[np.random.randint(len(far))]
    return np.exp2(a.ravel()).repeat(32)


def f64(x):
    return np.asarray(x).astype(np.float64)


def striped(idx):
    return np.tile(idx.reshape(-1, 16).T, (8, 1)).astype(np.uint16)


def unstriped(offs):
    return offs[:16].T.reshape(-1).astype(np.int64)


E2M1 = np.array([0.0, 0.5, 1.0, 1.5, 2.0, 3.0, 4.0, 6.0, -0.0, -0.5, -1.0, -1.5, -2.0, -3.0, -4.0, -6.0])


def pack_weight(w, fmt):
    k, n = w.shape
    w = f64(np.asarray(w, np.float32).astype(ml_dtypes.bfloat16)).reshape(k // 32, 32, n)
    amax = np.abs(w).max(1)
    if fmt == "e4m3":
        byte = np.frexp(amax)[1] - 1 + 127 - 7
    else:
        mant, ex = np.frexp(amax / 6.0)
        byte = np.where(mant > 0.5, ex, ex - 1) + 127
    byte = np.clip(np.where(amax > 0, byte, 1), 1, 254)
    scaled = (w * np.exp2(127.0 - byte)[:, None, :]).reshape(k, n).astype(np.float32)
    by_word = np.ascontiguousarray(scaled.reshape(k // 512, 128, 4, n).transpose(0, 1, 3, 2))
    if fmt == "e4m3":
        words = by_word.astype(ml_dtypes.float8_e4m3fn).view(np.uint8)
    else:
        c = by_word.astype(ml_dtypes.float4_e2m1fn).view(np.uint8) & 0xF
        words = (c[..., 0::2] | (c[..., 1::2] << 4)).reshape(k // 512, 128, 2 * n)
    return np.ascontiguousarray(words), np.ascontiguousarray(byte.astype(np.uint8).reshape(k // 512, 16, n))


def unpack_weight(words, scales, fmt):
    g, _, n = scales.shape
    words = np.ascontiguousarray(words).reshape(g, 128, n, -1)
    if fmt == "e4m3":
        vals = words.view(ml_dtypes.float8_e4m3fn).astype(np.float64)
    else:
        nib = np.empty((g, 128, n, 4), np.uint8)
        nib[..., 0::2] = words & 0xF
        nib[..., 1::2] = words >> 4
        vals = E2M1[nib]
    vals = vals * np.repeat(np.exp2(scales.astype(np.float64) - 127.0), 8, axis=1)[..., None]
    return vals.transpose(0, 1, 3, 2).reshape(g * 512, n)


def gelu(v):
    return 0.5 * v * (1.0 + np.tanh(np.sqrt(2.0 / np.pi) * (v + 0.044715 * v**3)))


K, H, N, M, T, T3, S, P = 1024, 1024, 512, 512, 4096, 2048, 1024, 512

def setup_inputs():
    n = np.random.standard_normal
    s = mx_kscale(K)[:, None]
    s2 = mx_kscale(M)[:, None]
    u = mx_kscale(H)[:, None]
    tab_words, tab_scales = pack_weight(n((K, T)) * s, "e4m3")
    tab2_words, tab2_scales = pack_weight(n((M, T3)) * s2, "e4m3")
    w1 = (1.5 * n((K, H)) / np.sqrt(K) / s).astype(np.float32)
    w2_words, w2_scales = pack_weight(1.3 * n((H, N)) / np.sqrt(H) / u, "e2m1")
    wp_words, wp_scales = pack_weight(n((M, N)) / np.sqrt(M) / s2, "e4m3")
    rel = (np.random.uniform(0.3, 1.7, (H, S)) * u).astype(np.float32)
    gate = np.random.uniform(0.4, 2.0, N).astype(np.float32)
    offs = striped(np.random.permutation(T)[:S])
    offs2 = striped(np.random.permutation(T3)[:P])
    pos1 = striped(np.random.permutation(S)[:P])
    return {"tab_words": tab_words, "tab_scales": tab_scales,
            "tab2_words": tab2_words, "tab2_scales": tab2_scales,
            "w1": w1, "w2_words": w2_words, "w2_scales": w2_scales,
            "wp_words": wp_words, "wp_scales": wp_scales,
            "rel": rel, "gate": gate,
            "offs": offs, "offs2": offs2, "pos1": pos1}

def reference(tab_words, tab_scales, tab2_words, tab2_scales, w1, w2_words, w2_scales,
              wp_words, wp_scales, rel, gate, offs, offs2, pos1):
    v = unpack_weight(tab_words, tab_scales, "e4m3")[:, unstriped(offs)]
    v2 = unpack_weight(tab2_words, tab2_scales, "e4m3")[:, unstriped(offs2)]
    w2 = unpack_weight(w2_words, w2_scales, "e2m1")
    wp = unpack_weight(wp_words, wp_scales, "e4m3")
    h = np.tanh(mxq(f64(w1), 0, "e4m3").T @ v) * f64(rel)
    y = w2.T @ mxq(h, 0, "e4m3")
    b = wp.T @ v2
    return np.abs(y[:, unstriped(pos1)] - b) * f64(gate)[:, None]

@@ -1,0 +1,238 @@
+from contextlib import ExitStack
+
+import concourse.mybir as mybir
+
+K, H, N, M, T, T3, S, PICK = 1024, 1024, 512, 512, 4096, 2048, 1024, 512
+FLOPS = 2 * (K * H * S + H * N * S + M * N * PICK)
+
+F32 = mybir.dt.float32
+BF16 = mybir.dt.bfloat16
+I32 = mybir.dt.int32
+U32 = mybir.dt.uint32
+U16 = mybir.dt.uint16
+U8 = mybir.dt.uint8
+FP8X4 = mybir.dt.float8_e4m3fn_x4
+FP4X4 = mybir.dt.float4_e2m1fn_x4
+ACT = mybir.ActivationFunctionType
+ALU = mybir.AluOpType
+
+P = 128
+PACK = 4
+PASS = P * PACK
+JC = 256
+TAB_PLANE = 4
+
+
+def tile_list_visit_deviation_review_kernel(
+    tc, tab_words, tab_scales, tab2_words, tab2_scales, w1, w2_words, w2_scales,
+    wp_words, wp_scales, rel, gate, offs, offs2, pos1, out,
+):
+    nc = tc.nc
+    with ExitStack() as ctx:
+        keep = ctx.enter_context(tc.tile_pool(name="keep", bufs=1))
+        ring = ctx.enter_context(tc.tile_pool(name="ring", bufs=2))
+        psum = ctx.enter_context(tc.psum_pool(name="psum", bufs=4))
+
+        idx = keep.tile([P, S // 16], U16, name="idx")
+        idx2 = keep.tile([P, PICK // 16], U16, name="idx2")
+        p1 = keep.tile([P, PICK // 16], U16, name="p1")
+        tab = [keep.tile([P, T], U32, name="tab%d" % a) for a in range(2)]
+        tab_sc = keep.tile([P, T], U8, name="tab_sc")
+        tab2 = keep.tile([P, T3], U32, name="tab2")
+        tab2_sc = keep.tile([P, T3], U8, name="tab2_sc")
+        w2 = keep.tile([P, 2, 2 * N], U8, name="w2", align_bytes=64)
+        w2_sc = keep.tile([P, 2, N], U8, name="w2_sc", align_bytes=64)
+        wp = keep.tile([P, N], U32, name="wp", align_bytes=64)
+        wp_sc = keep.tile([P, N], U8, name="wp_sc", align_bytes=64)
+        gate_col = keep.tile([P, N // P], F32, name="gate_col")
+        w1_raw = {(b, a): keep.tile([P, PACK, PASS], F32, name="w1_raw%d%d" % (b, a)) for b in range(2) for a in range(2)}
+        w1_q = {(b, a): keep.tile([P, PASS], U32, name="w1_q%d%d" % (b, a), align_bytes=64) for b in range(2) for a in range(2)}
+        w1_sc = {(b, a): keep.tile([P, PASS], U8, name="w1_sc%d%d" % (b, a), align_bytes=64) for b in range(2) for a in range(2)}
+        v = [keep.tile([P, S], U32, name="v%d" % a, align_bytes=64) for a in range(2)]
+        v_sc = keep.tile([P, S], U8, name="v_sc", align_bytes=64)
+        v2 = keep.tile([P, PICK], U32, name="v2", align_bytes=64)
+        v2_sc = keep.tile([P, PICK], U8, name="v2_sc", align_bytes=64)
+        y = [keep.tile([P, S], F32, name="y%d" % n) for n in range(N // P)]
+
+        nc.vector.memset(tab_sc[:].bitcast(I32), 0)
+        nc.vector.memset(tab2_sc[:].bitcast(I32), 0)
+        nc.vector.memset(w2_sc[:].rearrange("p a c -> p (a c)").bitcast(I32), 0)
+        nc.vector.memset(wp_sc[:].bitcast(I32), 0)
+
+        def load_w1(b, a):
+            rows = w1[a * PASS : (a + 1) * PASS, b * PASS : (b + 1) * PASS]
+            nc.sync.dma_start(out=w1_raw[b, a][:], in_=rows.rearrange("(p i) c -> p i c", i=PACK))
+
+        def load_words(tile, words):
+            nc.sync.dma_start(out=tile[:].bitcast(I32), in_=words.rearrange("p t i -> p (t i)").bitcast(I32))
+
+        rel_sb = {}
+
+        def load_rel(b, jc, chunks):
+            tile = keep.tile([P, PACK, chunks * JC], F32, name="rel%d%d" % (b, jc))
+            rows = rel[b * PASS : (b + 1) * PASS, jc * JC : (jc + chunks) * JC]
+            nc.sync.dma_start(out=tile[:], in_=rows.rearrange("(p t) j -> p t j", t=PACK))
+            for c in range(chunks):
+                rel_sb[b, jc + c] = tile[:, :, c * JC : (c + 1) * JC]
+
+        load_w1(0, 0)
+        for q in range(4):
+            nc.sync.dma_start(out=tab_sc[32 * q + TAB_PLANE : 32 * q + TAB_PLANE + 8, :].bitcast(I32),
+                              in_=tab_scales[:, 4 * q : 4 * q + 4, :].bitcast(I32))
+        nc.sync.dma_start(idx[:], offs)
+        load_w1(0, 1)
+        load_words(tab[0], tab_words[0])
+        nc.sync.dma_start(idx2[:], offs2)
+        for q in range(4):
+            nc.sync.dma_start(out=tab2_sc[32 * q : 32 * q + 4, :].bitcast(I32),
+                              in_=tab2_scales[0, 4 * q : 4 * q + 4, :].bitcast(I32))
+        load_words(tab[1], tab_words[1])
+        load_w1(1, 0)
+        load_w1(1, 1)
+        load_rel(0, 0, 1)
+        load_rel(0, 1, 1)
+        nc.sync.dma_start(out=w2[:].bitcast(I32), in_=w2_words.rearrange("a p c -> p a c").bitcast(I32))
+        for q in range(4):
+            nc.sync.dma_start(out=w2_sc[32 * q : 32 * q + 4, :, :].bitcast(I32),
+                              in_=w2_scales[:, 4 * q : 4 * q + 4, :].rearrange("a r c -> r a c").bitcast(I32))
+        load_rel(1, 0, 2)
+        load_rel(0, 2, 2)
+        load_rel(1, 2, 2)
+        load_words(tab2, tab2_words[0])
+        load_words(wp, wp_words[0])
+        for q in range(4):
+            nc.sync.dma_start(out=wp_sc[32 * q : 32 * q + 4, :].bitcast(I32),
+                              in_=wp_scales[0, 4 * q : 4 * q + 4, :].bitcast(I32))
+        nc.sync.dma_start(p1[:], pos1)
+        with nc.allow_non_contiguous_dma(reason="one gate value for each partition"):
+            nc.sync.dma_start(out=gate_col[:], in_=gate.rearrange("(n p) -> p n", p=P))
+
+        def quantise_w1(b, a, scalar_cols):
+            grouped = ring.tile([P, PACK * PASS], BF16, name="w1_grouped", align_bytes=64)
+            dst = grouped[:].rearrange("p (t m i) -> p m i t", t=PACK, i=PACK)
+            src = w1_raw[b, a][:].rearrange("p i (m t) -> p m i t", t=PACK)
+            if scalar_cols > 0:
+                nc.scalar.copy(out=dst[:, :scalar_cols], in_=src[:, :scalar_cols])
+            if scalar_cols < P:
+                nc.vector.tensor_copy(out=dst[:, scalar_cols:], in_=src[:, scalar_cols:])
+            nc.vector.quantize_mx(out=w1_q[b, a][:].bitcast(FP8X4), scales=w1_sc[b, a][:], in_=grouped[:])
+
+        def gather_v(a, half):
+            cols = slice(half * S // 2, (half + 1) * S // 2)
+            nc.vector.tensor_copy(out=v[a][:, cols], in_=tab[a][:].indirect(idx[:, half * 32 : (half + 1) * 32]))
+
+        tanh_sb = {}
+
+        def first_stage(b, jc):
+            cols = slice(jc * JC, (jc + 1) * JC)
+            th = ring.tile([P, PACK, JC], F32, name="th", bufs=5)
+            for g in range(2):
+                acc = psum.tile([P, 2, JC], F32, name="acc1", tag="wide")
+                for u in range(2):
+                    ch = slice((2 * g + u) * P, (2 * g + u + 1) * P)
+                    for a in range(2):
+                        nc.tensor.matmul_mx(
+                            out=acc[:, u, :],
+                            lhsT=w1_q[b, a][:, ch].bitcast(FP8X4), lhsT_scale=w1_sc[b, a][:, ch],
+                            rhs=v[a][:, cols].bitcast(FP8X4), rhs_scale=v_sc[TAB_PLANE + 4 * a :, cols],
+                            start=(a == 0), stop=(a == 1),
+                        )
+                nc.scalar.activation(out=th[:, 2 * g : 2 * g + 2, :], in_=acc[:], func=ACT.Tanh)
+            tanh_sb[b, jc] = th
+
+        h_bf, h_q, h_sc = {}, {}, {}
+
+        def weigh(b, jc):
+            hb = ring.tile([P, PACK * JC], BF16, name="h_bf", bufs=3, align_bytes=64)
+            nc.vector.tensor_tensor(
+                out=hb[:].rearrange("p (c e t) -> p c t e", e=2, t=PACK),
+                in0=tanh_sb[b, jc][:].rearrange("p t (c e) -> p c t e", e=2),
+                in1=rel_sb[b, jc].rearrange("p t (c e) -> p c t e", e=2),
+                op=ALU.mult,
+            )
+            h_bf[b, jc] = hb
+
+        def quantise_h(b, jc):
+            h_q[b, jc] = keep.tile([P, JC], U32, name="h_q%d%d" % (b, jc), align_bytes=64)
+            h_sc[b, jc] = keep.tile([P, JC], U8, name="h_sc%d%d" % (b, jc), align_bytes=64)
+            nc.vector.quantize_mx(out=h_q[b, jc][:].bitcast(FP8X4), scales=h_sc[b, jc][:], in_=h_bf[b, jc][:])
+
+        def second_stage(jc):
+            for n in range(N // P):
+                acc = psum.tile([P, JC], F32, name="acc2", tag="narrow")
+                for b in range(2):
+                    nc.tensor.matmul_mx(
+                        out=acc[:],
+                        lhsT=w2[:, b, 2 * n * P : 2 * (n + 1) * P].bitcast(FP4X4), lhsT_scale=w2_sc[:, b, n * P : (n + 1) * P],
+                        rhs=h_q[b, jc][:].bitcast(FP8X4), rhs_scale=h_sc[b, jc][:],
+                        start=(b == 0), stop=(b == 1),
+                    )
+                nc.scalar.copy(out=y[n][:, jc * JC : (jc + 1) * JC], in_=acc[:])
+
+        quantise_w1(0, 0, P)
+        nc.vector.tensor_copy(out=v_sc[:], in_=tab_sc[:].indirect(idx[:]))
+        quantise_w1(0, 1, P)
+        nc.vector.tensor_copy(out=v2_sc[:], in_=tab2_sc[:].indirect(idx2[:]))
+        for a in range(2):
+            for half in range(2):
+                gather_v(a, half)
+        first_stage(0, 0)
+        first_stage(0, 1)
+        quantise_w1(1, 0, 0)
+        quantise_w1(1, 1, P // 2)
+
+        units = [(b, 2 * jh + c) for jh in range(2) for b in range(2) for c in range(2)]
+        for i, (b, jc) in enumerate(units):
+            if i + 2 < len(units):
+                first_stage(*units[i + 2])
+            weigh(b, jc)
+            if i > 0:
+                pb, pjc = units[i - 1]
+                quantise_h(pb, pjc)
+                if pb == 1:
+                    second_stage(pjc)
+        quantise_h(*units[-1])
+        second_stage(units[-1][1])
+
+        nc.vector.tensor_copy(out=v2[:], in_=tab2[:].indirect(idx2[:]))
+        base = []
+        for n in range(N // P):
+            acc = psum.tile([P, PICK], F32, name="accb", tag="wide")
+            nc.tensor.matmul_mx(
+                out=acc[:],
+                lhsT=wp[:, n * P : (n + 1) * P].bitcast(FP8X4), lhsT_scale=wp_sc[:, n * P : (n + 1) * P],
+                rhs=v2[:].bitcast(FP8X4), rhs_scale=v2_sc[:],
+                start=True, stop=True,
+            )
+            base.append(acc)
+
+        pieces = [(n, 0, PICK) for n in range(N // P - 1)] + [(N // P - 1, 0, PICK // 2), (N // P - 1, PICK // 2, PICK)]
+        picked = {}
+
+        def pick(piece):
+            n, lo, hi = piece
+            picked[piece] = ring.tile([P, hi - lo], F32, name="picked")
+            nc.vector.tensor_copy(out=picked[piece][:], in_=y[n][:].indirect(p1[:, lo // 16 : hi // 16]))
+
+        def finish(piece, on_vector):
+            n, lo, hi = piece
+            diff = ring.tile([P, hi - lo], F32, name="diff")
+            nc.vector.tensor_tensor(out=diff[:], in0=picked[piece][:], in1=base[n][:, lo:hi], op=ALU.subtract)
+            size = ring.tile([P, hi - lo], F32, name="size")
+            nc.scalar.activation(out=size[:], in_=diff[:], func=ACT.Abs)
+            res = ring.tile([P, hi - lo], F32, name="res", bufs=3)
+            if on_vector:
+                late.append((piece, size, res))
+            else:
+                nc.scalar.activation(out=res[:], in_=size[:], func=ACT.Copy, scale=gate_col[:, n : n + 1])
+                nc.sync.dma_start(out=out[n * P : (n + 1) * P, lo:hi], in_=res[:])
+
+        late = []
+        pick(pieces[0])
+        for i, piece in enumerate(pieces):
+            if i + 1 < len(pieces):
+                pick(pieces[i + 1])
+            finish(piece, i >= len(pieces) - 2)
+        for (n, lo, hi), size, res in late:
+            nc.vector.tensor_scalar(out=res[:], in0=size[:], scalar1=gate_col[:, n : n + 1], scalar2=None, op0=ALU.mult)
+            nc.sync.dma_start(out=out[n * P : (n + 1) * P, lo:hi], in_=res[:])

@@ -21,6 +21,7 @@ PACK = 4
 PASS = P * PACK
 JC = 256
 TAB_PLANE = 4
+TAB2_PLANE = 12
 
 
 def tile_list_visit_deviation_review_kernel(
@@ -45,7 +46,7 @@ def tile_list_visit_deviation_review_kernel(
         wp = keep.tile([P, N], U32, name="wp", align_bytes=64)
         wp_sc = keep.tile([P, N], U8, name="wp_sc", align_bytes=64)
         gate_col = keep.tile([P, N // P], F32, name="gate_col")
-        w1_raw = {(b, a): keep.tile([P, PACK, PASS], F32, name="w1_raw%d%d" % (b, a)) for b in range(2) for a in range(2)}
+        w1_raw = {}
         w1_q = {(b, a): keep.tile([P, PASS], U32, name="w1_q%d%d" % (b, a), align_bytes=64) for b in range(2) for a in range(2)}
         w1_sc = {(b, a): keep.tile([P, PASS], U8, name="w1_sc%d%d" % (b, a), align_bytes=64) for b in range(2) for a in range(2)}
         v = [keep.tile([P, S], U32, name="v%d" % a, align_bytes=64) for a in range(2)]
@@ -53,68 +54,71 @@ def tile_list_visit_deviation_review_kernel(
         v2 = keep.tile([P, PICK], U32, name="v2", align_bytes=64)
         v2_sc = keep.tile([P, PICK], U8, name="v2_sc", align_bytes=64)
         y = [keep.tile([P, S], F32, name="y%d" % n) for n in range(N // P)]
+        base = [keep.tile([P, PICK], F32, name="base%d" % n) for n in range(N // P)]
 
         nc.vector.memset(tab_sc[:].bitcast(I32), 0)
         nc.vector.memset(tab2_sc[:].bitcast(I32), 0)
         nc.vector.memset(w2_sc[:].rearrange("p a c -> p (a c)").bitcast(I32), 0)
         nc.vector.memset(wp_sc[:].bitcast(I32), 0)
 
-        def load_w1(b, a):
-            rows = w1[a * PASS : (a + 1) * PASS, b * PASS : (b + 1) * PASS]
-            nc.sync.dma_start(out=w1_raw[b, a][:], in_=rows.rearrange("(p i) c -> p i c", i=PACK))
+        def load_w1(b, a, blocks):
+            tile = keep.tile([P, PACK, blocks * PASS], F32, name="w1_raw%d%d" % (b, a))
+            rows = w1[a * PASS : (a + 1) * PASS, b * PASS : (b + blocks) * PASS]
+            nc.sync.dma_start(out=tile[:], in_=rows.rearrange("(p i) c -> p i c", i=PACK))
+            for c in range(blocks):
+                w1_raw[b + c, a] = tile[:, :, c * PASS : (c + 1) * PASS]
 
         def load_words(tile, words):
             nc.sync.dma_start(out=tile[:].bitcast(I32), in_=words.rearrange("p t i -> p (t i)").bitcast(I32))
 
         rel_sb = {}
 
-        def load_rel(b, jc, chunks):
-            tile = keep.tile([P, PACK, chunks * JC], F32, name="rel%d%d" % (b, jc))
-            rows = rel[b * PASS : (b + 1) * PASS, jc * JC : (jc + chunks) * JC]
+        def load_rel(b, lo, hi):
+            tile = keep.tile([P, PACK, hi - lo], F32, name="rel%d_%d" % (b, lo))
+            rows = rel[b * PASS : (b + 1) * PASS, lo:hi]
             nc.sync.dma_start(out=tile[:], in_=rows.rearrange("(p t) j -> p t j", t=PACK))
-            for c in range(chunks):
-                rel_sb[b, jc + c] = tile[:, :, c * JC : (c + 1) * JC]
+            for c in range(lo, hi, P):
+                rel_sb[b, c] = (tile, c - lo)
 
-        load_w1(0, 0)
+        load_w1(0, 0, 1)
         for q in range(4):
             nc.sync.dma_start(out=tab_sc[32 * q + TAB_PLANE : 32 * q + TAB_PLANE + 8, :].bitcast(I32),
                               in_=tab_scales[:, 4 * q : 4 * q + 4, :].bitcast(I32))
         nc.sync.dma_start(idx[:], offs)
-        load_w1(0, 1)
+        load_w1(0, 1, 1)
         load_words(tab[0], tab_words[0])
         nc.sync.dma_start(idx2[:], offs2)
-        for q in range(4):
-            nc.sync.dma_start(out=tab2_sc[32 * q : 32 * q + 4, :].bitcast(I32),
-                              in_=tab2_scales[0, 4 * q : 4 * q + 4, :].bitcast(I32))
+        for r in range(4):
+            nc.sync.dma_start(out=tab2_sc[TAB2_PLANE + r : P : 32, :].bitcast(I32),
+                              in_=tab2_scales[0, r:16:4, :].bitcast(I32))
         load_words(tab[1], tab_words[1])
-        load_w1(1, 0)
-        load_w1(1, 1)
-        load_rel(0, 0, 1)
-        load_rel(0, 1, 1)
+        load_w1(1, 0, 1)
+        load_w1(1, 1, 1)
+        load_rel(0, 0, 512)
         nc.sync.dma_start(out=w2[:].bitcast(I32), in_=w2_words.rearrange("a p c -> p a c").bitcast(I32))
-        for q in range(4):
-            nc.sync.dma_start(out=w2_sc[32 * q : 32 * q + 4, :, :].bitcast(I32),
-                              in_=w2_scales[:, 4 * q : 4 * q + 4, :].rearrange("a r c -> r a c").bitcast(I32))
-        load_rel(1, 0, 2)
-        load_rel(0, 2, 2)
-        load_rel(1, 2, 2)
-        load_words(tab2, tab2_words[0])
+        for r in range(4):
+            nc.sync.dma_start(out=w2_sc[r:P:32, :, :].bitcast(I32),
+                              in_=w2_scales[:, r:16:4, :].rearrange("a q c -> q a c").bitcast(I32))
+        load_rel(1, 0, 512)
+        load_rel(0, 512, 1024)
+        load_rel(1, 512, 896)
         load_words(wp, wp_words[0])
-        for q in range(4):
-            nc.sync.dma_start(out=wp_sc[32 * q : 32 * q + 4, :].bitcast(I32),
-                              in_=wp_scales[0, 4 * q : 4 * q + 4, :].bitcast(I32))
+        for r in range(4):
+            nc.sync.dma_start(out=wp_sc[r:P:32, :].bitcast(I32), in_=wp_scales[0, r:16:4, :].bitcast(I32))
+        load_words(tab2, tab2_words[0])
+        load_rel(1, 896, 1024)
         nc.sync.dma_start(p1[:], pos1)
         with nc.allow_non_contiguous_dma(reason="one gate value for each partition"):
             nc.sync.dma_start(out=gate_col[:], in_=gate.rearrange("(n p) -> p n", p=P))
 
         def quantise_w1(b, a, scalar_cols):
             grouped = ring.tile([P, PACK * PASS], BF16, name="w1_grouped", align_bytes=64)
-            dst = grouped[:].rearrange("p (t m i) -> p m i t", t=PACK, i=PACK)
-            src = w1_raw[b, a][:].rearrange("p i (m t) -> p m i t", t=PACK)
+            dst = grouped[:].rearrange("p (u e m i) -> p u m i e", u=2, e=2, i=PACK)
+            src = w1_raw[b, a].rearrange("p i (m u e) -> p u m i e", u=2, e=2)
             if scalar_cols > 0:
-                nc.scalar.copy(out=dst[:, :scalar_cols], in_=src[:, :scalar_cols])
+                nc.scalar.copy(out=dst[:, :, :scalar_cols], in_=src[:, :, :scalar_cols])
             if scalar_cols < P:
-                nc.vector.tensor_copy(out=dst[:, scalar_cols:], in_=src[:, scalar_cols:])
+                nc.vector.tensor_copy(out=dst[:, :, scalar_cols:], in_=src[:, :, scalar_cols:])
             nc.vector.quantize_mx(out=w1_q[b, a][:].bitcast(FP8X4), scales=w1_sc[b, a][:], in_=grouped[:])
 
         def gather_v(a, half):
@@ -140,34 +144,53 @@ def tile_list_visit_deviation_review_kernel(
                 nc.scalar.activation(out=th[:, 2 * g : 2 * g + 2, :], in_=acc[:], func=ACT.Tanh)
             tanh_sb[b, jc] = th
 
-        h_bf, h_q, h_sc = {}, {}, {}
+        h_bf, h_q = {}, {}
 
-        def weigh(b, jc):
-            hb = ring.tile([P, PACK * JC], BF16, name="h_bf", bufs=3, align_bytes=64)
+        def weigh(b, lo, hi):
+            hb = ring.tile([P, PACK * (hi - lo)], BF16, name="h_bf", bufs=3, align_bytes=64)
+            rel_tile, rel_lo = rel_sb[b, lo]
             nc.vector.tensor_tensor(
                 out=hb[:].rearrange("p (c e t) -> p c t e", e=2, t=PACK),
-                in0=tanh_sb[b, jc][:].rearrange("p t (c e) -> p c t e", e=2),
-                in1=rel_sb[b, jc].rearrange("p t (c e) -> p c t e", e=2),
+                in0=tanh_sb[b, lo // JC][:, :, lo % JC : lo % JC + hi - lo].rearrange("p t (c e) -> p c t e", e=2),
+                in1=rel_tile[:, :, rel_lo : rel_lo + hi - lo].rearrange("p t (c e) -> p c t e", e=2),
                 op=ALU.mult,
             )
-            h_bf[b, jc] = hb
+            h_bf[b, lo] = hb
 
-        def quantise_h(b, jc):
-            h_q[b, jc] = keep.tile([P, JC], U32, name="h_q%d%d" % (b, jc), align_bytes=64)
-            h_sc[b, jc] = keep.tile([P, JC], U8, name="h_sc%d%d" % (b, jc), align_bytes=64)
-            nc.vector.quantize_mx(out=h_q[b, jc][:].bitcast(FP8X4), scales=h_sc[b, jc][:], in_=h_bf[b, jc][:])
+        def quantise_h(b, lo, hi):
+            codes = keep.tile([P, hi - lo], U32, name="h_q%d_%d" % (b, lo), align_bytes=64)
+            scales = keep.tile([P, hi - lo], U8, name="h_sc%d_%d" % (b, lo), align_bytes=64)
+            nc.vector.quantize_mx(out=codes[:].bitcast(FP8X4), scales=scales[:], in_=h_bf[b, lo][:])
+            for c in range(lo, hi, P):
+                h_q[b, c] = (codes, scales, c - lo)
 
-        def second_stage(jc):
+        def second_stage(lo, hi):
             for n in range(N // P):
-                acc = psum.tile([P, JC], F32, name="acc2", tag="narrow")
+                acc = psum.tile([P, hi - lo], F32, name="acc2", tag="narrow")
                 for b in range(2):
+                    codes, scales, first = h_q[b, lo]
+                    cols = slice(first, first + hi - lo)
                     nc.tensor.matmul_mx(
                         out=acc[:],
                         lhsT=w2[:, b, 2 * n * P : 2 * (n + 1) * P].bitcast(FP4X4), lhsT_scale=w2_sc[:, b, n * P : (n + 1) * P],
-                        rhs=h_q[b, jc][:].bitcast(FP8X4), rhs_scale=h_sc[b, jc][:],
+                        rhs=codes[:, cols].bitcast(FP8X4), rhs_scale=scales[:, cols],
                         start=(b == 0), stop=(b == 1),
                     )
-                nc.scalar.copy(out=y[n][:, jc * JC : (jc + 1) * JC], in_=acc[:])
+                nc.scalar.copy(out=y[n][:, lo:hi], in_=acc[:])
+
+        def expected():
+            nc.vector.tensor_copy(out=v2[:], in_=tab2[:].indirect(idx2[:]))
+            banks = []
+            for n in range(N // P):
+                acc = psum.tile([P, PICK], F32, name="accb", tag="wide")
+                nc.tensor.matmul_mx(
+                    out=acc[:],
+                    lhsT=wp[:, n * P : (n + 1) * P].bitcast(FP8X4), lhsT_scale=wp_sc[:, n * P : (n + 1) * P],
+                    rhs=v2[:].bitcast(FP8X4), rhs_scale=v2_sc[TAB2_PLANE:, :],
+                    start=True, stop=True,
+                )
+                banks.append(acc)
+            return banks
 
         quantise_w1(0, 0, P)
         nc.vector.tensor_copy(out=v_sc[:], in_=tab_sc[:].indirect(idx[:]))
@@ -179,60 +202,40 @@ def tile_list_visit_deviation_review_kernel(
         first_stage(0, 0)
         first_stage(0, 1)
         quantise_w1(1, 0, 0)
-        quantise_w1(1, 1, P // 2)
+        quantise_w1(1, 1, 0)
 
-        units = [(b, 2 * jh + c) for jh in range(2) for b in range(2) for c in range(2)]
-        for i, (b, jc) in enumerate(units):
-            if i + 2 < len(units):
-                first_stage(*units[i + 2])
-            weigh(b, jc)
+        tanh_units = [(b, 2 * jh + c) for jh in range(2) for b in range(2) for c in range(2)]
+        units = [(b, jc * JC, (jc + 1) * JC) for b, jc in tanh_units[:-1]] + [(1, S - JC, S - P), (1, S - P, S)]
+        for i, unit in enumerate(units):
+            if i + 2 < len(tanh_units):
+                first_stage(*tanh_units[i + 2])
+            if i == len(units) - 1:
+                banks = expected()
+                for n in range(2):
+                    nc.scalar.copy(out=base[n][:], in_=banks[n][:])
+            weigh(*unit)
             if i > 0:
-                pb, pjc = units[i - 1]
-                quantise_h(pb, pjc)
-                if pb == 1:
-                    second_stage(pjc)
+                quantise_h(*units[i - 1])
+                if units[i - 1][0] == 1:
+                    second_stage(*units[i - 1][1:])
         quantise_h(*units[-1])
-        second_stage(units[-1][1])
-
-        nc.vector.tensor_copy(out=v2[:], in_=tab2[:].indirect(idx2[:]))
-        base = []
-        for n in range(N // P):
-            acc = psum.tile([P, PICK], F32, name="accb", tag="wide")
-            nc.tensor.matmul_mx(
-                out=acc[:],
-                lhsT=wp[:, n * P : (n + 1) * P].bitcast(FP8X4), lhsT_scale=wp_sc[:, n * P : (n + 1) * P],
-                rhs=v2[:].bitcast(FP8X4), rhs_scale=v2_sc[:],
-                start=True, stop=True,
-            )
-            base.append(acc)
+        second_stage(*units[-1][1:])
+        for n in range(2, 4):
+            nc.vector.tensor_copy(out=base[n][:], in_=banks[n][:])
 
         pieces = [(n, 0, PICK) for n in range(N // P - 1)] + [(N // P - 1, 0, PICK // 2), (N // P - 1, PICK // 2, PICK)]
-        picked = {}
-
-        def pick(piece):
-            n, lo, hi = piece
-            picked[piece] = ring.tile([P, hi - lo], F32, name="picked")
-            nc.vector.tensor_copy(out=picked[piece][:], in_=y[n][:].indirect(p1[:, lo // 16 : hi // 16]))
-
-        def finish(piece, on_vector):
-            n, lo, hi = piece
-            diff = ring.tile([P, hi - lo], F32, name="diff")
-            nc.vector.tensor_tensor(out=diff[:], in0=picked[piece][:], in1=base[n][:, lo:hi], op=ALU.subtract)
+        late = []
+        for i, (n, lo, hi) in enumerate(pieces):
+            diff = ring.tile([P, hi - lo], F32, name="diff", bufs=3)
+            nc.vector.tensor_tensor(out=diff[:], in0=y[n][:].indirect(p1[:, lo // 16 : hi // 16]), in1=base[n][:, lo:hi], op=ALU.subtract)
             size = ring.tile([P, hi - lo], F32, name="size")
             nc.scalar.activation(out=size[:], in_=diff[:], func=ACT.Abs)
             res = ring.tile([P, hi - lo], F32, name="res", bufs=3)
-            if on_vector:
-                late.append((piece, size, res))
+            if i >= len(pieces) - 2:
+                late.append((n, lo, hi, size, res))
             else:
                 nc.scalar.activation(out=res[:], in_=size[:], func=ACT.Copy, scale=gate_col[:, n : n + 1])
                 nc.sync.dma_start(out=out[n * P : (n + 1) * P, lo:hi], in_=res[:])
-
-        late = []
-        pick(pieces[0])
-        for i, piece in enumerate(pieces):
-            if i + 1 < len(pieces):
-                pick(pieces[i + 1])
-            finish(piece, i >= len(pieces) - 2)
-        for (n, lo, hi), size, res in late:
+        for n, lo, hi, size, res in late:
             nc.vector.tensor_scalar(out=res[:], in0=size[:], scalar1=gate_col[:, n : n + 1], scalar2=None, op0=ALU.mult)
             nc.sync.dma_start(out=out[n * P : (n + 1) * P, lo:hi], in_=res[:])

@@ -51,7 +51,6 @@ def tile_list_visit_deviation_review_kernel(
         w1_sc = {(b, a): keep.tile([P, PASS], U8, name="w1_sc%d%d" % (b, a), align_bytes=64) for b in range(2) for a in range(2)}
         v = [keep.tile([P, S], U32, name="v%d" % a, align_bytes=64) for a in range(2)]
         v_sc = keep.tile([P, S], U8, name="v_sc", align_bytes=64)
-        v2 = keep.tile([P, PICK], U32, name="v2", align_bytes=64)
         v2_sc = keep.tile([P, PICK], U8, name="v2_sc", align_bytes=64)
         y = [keep.tile([P, S], F32, name="y%d" % n) for n in range(N // P)]
         base = [keep.tile([P, PICK], F32, name="base%d" % n) for n in range(N // P)]
@@ -61,12 +60,11 @@ def tile_list_visit_deviation_review_kernel(
         nc.vector.memset(w2_sc[:].rearrange("p a c -> p (a c)").bitcast(I32), 0)
         nc.vector.memset(wp_sc[:].bitcast(I32), 0)
 
-        def load_w1(b, a, blocks):
-            tile = keep.tile([P, PACK, blocks * PASS], F32, name="w1_raw%d%d" % (b, a))
-            rows = w1[a * PASS : (a + 1) * PASS, b * PASS : (b + blocks) * PASS]
-            nc.sync.dma_start(out=tile[:], in_=rows.rearrange("(p i) c -> p i c", i=PACK))
-            for c in range(blocks):
-                w1_raw[b + c, a] = tile[:, :, c * PASS : (c + 1) * PASS]
+        def load_w1(a):
+            tile = keep.tile([P, PACK, H], F32, name="w1_raw%d" % a)
+            nc.sync.dma_start(out=tile[:], in_=w1[a * PASS : (a + 1) * PASS, :].rearrange("(p i) c -> p i c", i=PACK))
+            for b in range(2):
+                w1_raw[b, a] = tile[:, :, b * PASS : (b + 1) * PASS]
 
         def load_words(tile, words):
             nc.sync.dma_start(out=tile[:].bitcast(I32), in_=words.rearrange("p t i -> p (t i)").bitcast(I32))
@@ -74,32 +72,35 @@ def tile_list_visit_deviation_review_kernel(
         rel_sb = {}
 
         def load_rel(b, lo, hi):
-            tile = keep.tile([P, PACK, hi - lo], F32, name="rel%d_%d" % (b, lo))
+            tile = keep.tile([P, PACK, hi - lo], F32, name="rel%d_%d" % (b, lo), align_bytes=64)
             rows = rel[b * PASS : (b + 1) * PASS, lo:hi]
             nc.sync.dma_start(out=tile[:], in_=rows.rearrange("(p t) j -> p t j", t=PACK))
             for c in range(lo, hi, P):
                 rel_sb[b, c] = (tile, c - lo)
 
-        load_w1(0, 0, 1)
-        for q in range(4):
-            nc.sync.dma_start(out=tab_sc[32 * q + TAB_PLANE : 32 * q + TAB_PLANE + 8, :].bitcast(I32),
-                              in_=tab_scales[:, 4 * q : 4 * q + 4, :].bitcast(I32))
+        def load_tab_scales(rows):
+            for r in rows:
+                for a in range(2):
+                    nc.sync.dma_start(out=tab_sc[TAB_PLANE + 4 * a + r : P : 32, :].bitcast(I32),
+                                      in_=tab_scales[a, r:16:4, :].bitcast(I32))
+
+        load_w1(0)
+        load_tab_scales(range(0, 2))
+        load_w1(1)
+        load_tab_scales(range(2, 4))
         nc.sync.dma_start(idx[:], offs)
-        load_w1(0, 1, 1)
         load_words(tab[0], tab_words[0])
         nc.sync.dma_start(idx2[:], offs2)
         for r in range(4):
             nc.sync.dma_start(out=tab2_sc[TAB2_PLANE + r : P : 32, :].bitcast(I32),
                               in_=tab2_scales[0, r:16:4, :].bitcast(I32))
         load_words(tab[1], tab_words[1])
-        load_w1(1, 0, 1)
-        load_w1(1, 1, 1)
         load_rel(0, 0, 512)
+        load_rel(1, 0, 512)
         nc.sync.dma_start(out=w2[:].bitcast(I32), in_=w2_words.rearrange("a p c -> p a c").bitcast(I32))
         for r in range(4):
             nc.sync.dma_start(out=w2_sc[r:P:32, :, :].bitcast(I32),
                               in_=w2_scales[:, r:16:4, :].rearrange("a q c -> q a c").bitcast(I32))
-        load_rel(1, 0, 512)
         load_rel(0, 512, 1024)
         load_rel(1, 512, 896)
         load_words(wp, wp_words[0])
@@ -111,7 +112,9 @@ def tile_list_visit_deviation_review_kernel(
         with nc.allow_non_contiguous_dma(reason="one gate value for each partition"):
             nc.sync.dma_start(out=gate_col[:], in_=gate.rearrange("(n p) -> p n", p=P))
 
-        def quantise_w1(b, a, scalar_cols):
+        w1_bf = {}
+
+        def round_w1(b, a, scalar_cols):
             grouped = ring.tile([P, PACK * PASS], BF16, name="w1_grouped", align_bytes=64)
             dst = grouped[:].rearrange("p (u e m i) -> p u m i e", u=2, e=2, i=PACK)
             src = w1_raw[b, a].rearrange("p i (m u e) -> p u m i e", u=2, e=2)
@@ -119,39 +122,44 @@ def tile_list_visit_deviation_review_kernel(
                 nc.scalar.copy(out=dst[:, :, :scalar_cols], in_=src[:, :, :scalar_cols])
             if scalar_cols < P:
                 nc.vector.tensor_copy(out=dst[:, :, scalar_cols:], in_=src[:, :, scalar_cols:])
-            nc.vector.quantize_mx(out=w1_q[b, a][:].bitcast(FP8X4), scales=w1_sc[b, a][:], in_=grouped[:])
+            w1_bf[b, a] = grouped
 
-        def gather_v(a, half):
-            cols = slice(half * S // 2, (half + 1) * S // 2)
-            nc.vector.tensor_copy(out=v[a][:, cols], in_=tab[a][:].indirect(idx[:, half * 32 : (half + 1) * 32]))
+        def quantise_w1(b, a):
+            nc.vector.quantize_mx(out=w1_q[b, a][:].bitcast(FP8X4), scales=w1_sc[b, a][:], in_=w1_bf[b, a][:])
+
+        def gather_v(a, lo, hi):
+            nc.vector.tensor_copy(out=v[a][:, lo:hi], in_=tab[a][:].indirect(idx[:, lo // 16 : hi // 16]))
 
         tanh_sb = {}
 
-        def first_stage(b, jc):
-            cols = slice(jc * JC, (jc + 1) * JC)
-            th = ring.tile([P, PACK, JC], F32, name="th", bufs=5)
-            for g in range(2):
-                acc = psum.tile([P, 2, JC], F32, name="acc1", tag="wide")
-                for u in range(2):
-                    ch = slice((2 * g + u) * P, (2 * g + u + 1) * P)
-                    for a in range(2):
+        def first_stage(b, lo, hi, tag):
+            width = hi - lo
+            th = keep.tile([P, PACK, width], F32, name="th", tag=tag)
+            per_bank = PASS // width
+            for t0 in range(0, PACK, per_bank):
+                acc = psum.tile([P, per_bank, width], F32, name="acc1", tag="wide")
+                for a in range(2):
+                    for u in range(per_bank):
+                        ch = slice((t0 + u) * P, (t0 + u + 1) * P)
                         nc.tensor.matmul_mx(
                             out=acc[:, u, :],
                             lhsT=w1_q[b, a][:, ch].bitcast(FP8X4), lhsT_scale=w1_sc[b, a][:, ch],
-                            rhs=v[a][:, cols].bitcast(FP8X4), rhs_scale=v_sc[TAB_PLANE + 4 * a :, cols],
-                            start=(a == 0), stop=(a == 1),
+                            rhs=v[a][:, lo:hi].bitcast(FP8X4), rhs_scale=v_sc[TAB_PLANE + 4 * a :, lo:hi],
+                            start=(a == 0 and u == 0), stop=(a == 1 and u == per_bank - 1),
                         )
-                nc.scalar.activation(out=th[:, 2 * g : 2 * g + 2, :], in_=acc[:], func=ACT.Tanh)
-            tanh_sb[b, jc] = th
+                nc.scalar.activation(out=th[:, t0 : t0 + per_bank, :], in_=acc[:], func=ACT.Tanh)
+            for c in range(lo, hi, P):
+                tanh_sb[b, c] = (th, c - lo)
 
         h_bf, h_q = {}, {}
 
         def weigh(b, lo, hi):
             hb = ring.tile([P, PACK * (hi - lo)], BF16, name="h_bf", bufs=3, align_bytes=64)
             rel_tile, rel_lo = rel_sb[b, lo]
+            th, th_lo = tanh_sb[b, lo]
             nc.vector.tensor_tensor(
                 out=hb[:].rearrange("p (c e t) -> p c t e", e=2, t=PACK),
-                in0=tanh_sb[b, lo // JC][:, :, lo % JC : lo % JC + hi - lo].rearrange("p t (c e) -> p c t e", e=2),
+                in0=th[:, :, th_lo : th_lo + hi - lo].rearrange("p t (c e) -> p c t e", e=2),
                 in1=rel_tile[:, :, rel_lo : rel_lo + hi - lo].rearrange("p t (c e) -> p c t e", e=2),
                 op=ALU.mult,
             )
@@ -164,21 +172,27 @@ def tile_list_visit_deviation_review_kernel(
             for c in range(lo, hi, P):
                 h_q[b, c] = (codes, scales, c - lo)
 
+        y_banks = {}
+
         def second_stage(lo, hi):
+            half, at = divmod(lo, PASS)
             for n in range(N // P):
-                acc = psum.tile([P, hi - lo], F32, name="acc2", tag="narrow")
+                if at == 0:
+                    y_banks[n] = psum.tile([P, PASS], F32, name="acc2", tag="second")
                 for b in range(2):
                     codes, scales, first = h_q[b, lo]
                     cols = slice(first, first + hi - lo)
                     nc.tensor.matmul_mx(
-                        out=acc[:],
+                        out=y_banks[n][:, at : at + hi - lo],
                         lhsT=w2[:, b, 2 * n * P : 2 * (n + 1) * P].bitcast(FP4X4), lhsT_scale=w2_sc[:, b, n * P : (n + 1) * P],
                         rhs=codes[:, cols].bitcast(FP8X4), rhs_scale=scales[:, cols],
                         start=(b == 0), stop=(b == 1),
                     )
-                nc.scalar.copy(out=y[n][:, lo:hi], in_=acc[:])
+                if hi % PASS == 0:
+                    nc.scalar.copy(out=y[n][:, half * PASS : (half + 1) * PASS], in_=y_banks[n][:])
 
         def expected():
+            v2 = keep.tile([P, PICK], U32, name="v2", tag="rel1_512", align_bytes=64)
             nc.vector.tensor_copy(out=v2[:], in_=tab2[:].indirect(idx2[:]))
             banks = []
             for n in range(N // P):
@@ -192,46 +206,53 @@ def tile_list_visit_deviation_review_kernel(
                 banks.append(acc)
             return banks
 
-        quantise_w1(0, 0, P)
-        nc.vector.tensor_copy(out=v_sc[:], in_=tab_sc[:].indirect(idx[:]))
-        quantise_w1(0, 1, P)
-        nc.vector.tensor_copy(out=v2_sc[:], in_=tab2_sc[:].indirect(idx2[:]))
         for a in range(2):
-            for half in range(2):
-                gather_v(a, half)
-        first_stage(0, 0)
-        first_stage(0, 1)
-        quantise_w1(1, 0, 0)
-        quantise_w1(1, 1, 0)
+            round_w1(0, a, P)
+            round_w1(1, a, 0)
+            quantise_w1(1, a)
+            quantise_w1(0, a)
+        nc.vector.tensor_copy(out=v_sc[:], in_=tab_sc[:].indirect(idx[:]))
+        gather_v(0, 0, S)
+        nc.vector.tensor_copy(out=v2_sc[:], in_=tab2_sc[:].indirect(idx2[:]))
+        gather_v(1, 0, JC)
+        gather_v(1, JC, 2 * JC)
+        gather_v(1, 2 * JC, S)
+        first_stage(0, 0, 256, "th0")
+        first_stage(0, 256, 512, "th1")
+        first_stage(1, 0, 512, "w1_raw0")
+        first_stage(0, 512, 1024, "w1_raw1")
+        first_stage(1, 512, 1024, "th2")
 
-        tanh_units = [(b, 2 * jh + c) for jh in range(2) for b in range(2) for c in range(2)]
-        units = [(b, jc * JC, (jc + 1) * JC) for b, jc in tanh_units[:-1]] + [(1, S - JC, S - P), (1, S - P, S)]
-        for i, unit in enumerate(units):
-            if i + 2 < len(tanh_units):
-                first_stage(*tanh_units[i + 2])
-            if i == len(units) - 1:
-                banks = expected()
-                for n in range(2):
-                    nc.scalar.copy(out=base[n][:], in_=banks[n][:])
+        units = [(0, 0, 256), (0, 256, 512), (1, 0, 512), (0, 512, 1024), (1, 512, 768), (1, 768, 896), (1, 896, 1024)]
+
+        def close(unit):
+            quantise_h(*unit)
+            if unit[0] == 1:
+                for lo in range(unit[1], unit[2], JC):
+                    second_stage(lo, min(lo + JC, unit[2]))
+
+        for i, unit in enumerate(units[:-1]):
             weigh(*unit)
             if i > 0:
-                quantise_h(*units[i - 1])
-                if units[i - 1][0] == 1:
-                    second_stage(*units[i - 1][1:])
-        quantise_h(*units[-1])
-        second_stage(*units[-1][1:])
-        for n in range(2, 4):
-            nc.vector.tensor_copy(out=base[n][:], in_=banks[n][:])
+                close(units[i - 1])
+        banks = expected()
+        for n in range(2):
+            nc.scalar.copy(out=base[n][:], in_=banks[n][:])
+        close(units[-2])
+        weigh(*units[-1])
+        nc.vector.tensor_copy(out=base[2][:], in_=banks[2][:])
+        close(units[-1])
+        nc.vector.tensor_copy(out=base[3][:], in_=banks[3][:])
 
         pieces = [(n, 0, PICK) for n in range(N // P - 1)] + [(N // P - 1, 0, PICK // 2), (N // P - 1, PICK // 2, PICK)]
         late = []
         for i, (n, lo, hi) in enumerate(pieces):
             diff = ring.tile([P, hi - lo], F32, name="diff", bufs=3)
             nc.vector.tensor_tensor(out=diff[:], in0=y[n][:].indirect(p1[:, lo // 16 : hi // 16]), in1=base[n][:, lo:hi], op=ALU.subtract)
-            size = ring.tile([P, hi - lo], F32, name="size")
+            size = ring.tile([P, hi - lo], F32, name="size", bufs=3)
             nc.scalar.activation(out=size[:], in_=diff[:], func=ACT.Abs)
-            res = ring.tile([P, hi - lo], F32, name="res", bufs=3)
-            if i >= len(pieces) - 2:
+            res = ring.tile([P, hi - lo], F32, name="res", bufs=5)
+            if i >= len(pieces) - 3:
                 late.append((n, lo, hi, size, res))
             else:
                 nc.scalar.activation(out=res[:], in_=size[:], func=ACT.Copy, scale=gate_col[:, n : n + 1])

from contextlib import ExitStack

import concourse.mybir as mybir

K, H, N, M, T, T3, S, PICK = 1024, 1024, 512, 512, 4096, 2048, 1024, 512
FLOPS = 2 * (K * H * S + H * N * S + M * N * PICK)

F32 = mybir.dt.float32
BF16 = mybir.dt.bfloat16
I32 = mybir.dt.int32
U32 = mybir.dt.uint32
U16 = mybir.dt.uint16
U8 = mybir.dt.uint8
FP8X4 = mybir.dt.float8_e4m3fn_x4
FP4X4 = mybir.dt.float4_e2m1fn_x4
ACT = mybir.ActivationFunctionType
ALU = mybir.AluOpType

P = 128
PACK = 4
PASS = P * PACK
JC = 256
TAB_PLANE = 4
TAB2_PLANE = 12


def tile_list_visit_deviation_review_kernel(
    tc, tab_words, tab_scales, tab2_words, tab2_scales, w1, w2_words, w2_scales,
    wp_words, wp_scales, rel, gate, offs, offs2, pos1, out,
):
    nc = tc.nc
    with ExitStack() as ctx:
        keep = ctx.enter_context(tc.tile_pool(name="keep", bufs=1))
        ring = ctx.enter_context(tc.tile_pool(name="ring", bufs=2))
        psum = ctx.enter_context(tc.psum_pool(name="psum", bufs=4))

        idx = keep.tile([P, S // 16], U16, name="idx")
        idx2 = keep.tile([P, PICK // 16], U16, name="idx2")
        p1 = keep.tile([P, PICK // 16], U16, name="p1")
        tab = [keep.tile([P, T], U32, name="tab%d" % a) for a in range(2)]
        tab_sc = keep.tile([P, T], U8, name="tab_sc")
        tab2 = keep.tile([P, T3], U32, name="tab2")
        tab2_sc = keep.tile([P, T3], U8, name="tab2_sc")
        w2 = keep.tile([P, 2, 2 * N], U8, name="w2", align_bytes=64)
        w2_sc = keep.tile([P, 2, N], U8, name="w2_sc", align_bytes=64)
        wp = keep.tile([P, N], U32, name="wp", align_bytes=64)
        wp_sc = keep.tile([P, N], U8, name="wp_sc", align_bytes=64)
        gate_col = keep.tile([P, N // P], F32, name="gate_col")
        w1_raw = {}
        w1_q = {(b, a): keep.tile([P, PASS], U32, name="w1_q%d%d" % (b, a), align_bytes=64) for b in range(2) for a in range(2)}
        w1_sc = {(b, a): keep.tile([P, PASS], U8, name="w1_sc%d%d" % (b, a), align_bytes=64) for b in range(2) for a in range(2)}
        v = [keep.tile([P, S], U32, name="v%d" % a, align_bytes=64) for a in range(2)]
        v_sc = keep.tile([P, S], U8, name="v_sc", align_bytes=64)
        v2_sc = keep.tile([P, PICK], U8, name="v2_sc", align_bytes=64)
        y = [keep.tile([P, S], F32, name="y%d" % n) for n in range(N // P)]
        base = [keep.tile([P, PICK], F32, name="base%d" % n) for n in range(N // P)]

        nc.vector.memset(tab_sc[:].bitcast(I32), 0)
        nc.vector.memset(tab2_sc[:].bitcast(I32), 0)
        nc.vector.memset(w2_sc[:].rearrange("p a c -> p (a c)").bitcast(I32), 0)
        nc.vector.memset(wp_sc[:].bitcast(I32), 0)

        def load_w1(a):
            tile = keep.tile([P, PACK, H], F32, name="w1_raw%d" % a)
            nc.sync.dma_start(out=tile[:], in_=w1[a * PASS : (a + 1) * PASS, :].rearrange("(p i) c -> p i c", i=PACK))
            for b in range(2):
                w1_raw[b, a] = tile[:, :, b * PASS : (b + 1) * PASS]

        def load_words(tile, words):
            nc.sync.dma_start(out=tile[:].bitcast(I32), in_=words.rearrange("p t i -> p (t i)").bitcast(I32))

        rel_sb = {}

        def load_rel(b, lo, hi):
            tile = keep.tile([P, PACK, hi - lo], F32, name="rel%d_%d" % (b, lo), align_bytes=64)
            rows = rel[b * PASS : (b + 1) * PASS, lo:hi]
            nc.sync.dma_start(out=tile[:], in_=rows.rearrange("(p t) j -> p t j", t=PACK))
            for c in range(lo, hi, P):
                rel_sb[b, c] = (tile, c - lo)

        def load_tab_scales(rows):
            for r in rows:
                for a in range(2):
                    nc.sync.dma_start(out=tab_sc[TAB_PLANE + 4 * a + r : P : 32, :].bitcast(I32),
                                      in_=tab_scales[a, r:16:4, :].bitcast(I32))

        load_w1(0)
        load_tab_scales(range(0, 2))
        load_w1(1)
        load_tab_scales(range(2, 4))
        nc.sync.dma_start(idx[:], offs)
        load_words(tab[0], tab_words[0])
        nc.sync.dma_start(idx2[:], offs2)
        for r in range(4):
            nc.sync.dma_start(out=tab2_sc[TAB2_PLANE + r : P : 32, :].bitcast(I32),
                              in_=tab2_scales[0, r:16:4, :].bitcast(I32))
        load_words(tab[1], tab_words[1])
        load_rel(0, 0, 512)
        load_rel(1, 0, 512)
        nc.sync.dma_start(out=w2[:].bitcast(I32), in_=w2_words.rearrange("a p c -> p a c").bitcast(I32))
        for r in range(4):
            nc.sync.dma_start(out=w2_sc[r:P:32, :, :].bitcast(I32),
                              in_=w2_scales[:, r:16:4, :].rearrange("a q c -> q a c").bitcast(I32))
        load_rel(0, 512, 1024)
        load_rel(1, 512, 896)
        load_words(wp, wp_words[0])
        for r in range(4):
            nc.sync.dma_start(out=wp_sc[r:P:32, :].bitcast(I32), in_=wp_scales[0, r:16:4, :].bitcast(I32))
        load_words(tab2, tab2_words[0])
        load_rel(1, 896, 1024)
        nc.sync.dma_start(p1[:], pos1)
        with nc.allow_non_contiguous_dma(reason="one gate value for each partition"):
            nc.sync.dma_start(out=gate_col[:], in_=gate.rearrange("(n p) -> p n", p=P))

        w1_bf = {}

        def round_w1(b, a, scalar_cols):
            grouped = ring.tile([P, PACK * PASS], BF16, name="w1_grouped", align_bytes=64)
            dst = grouped[:].rearrange("p (u e m i) -> p u m i e", u=2, e=2, i=PACK)
            src = w1_raw[b, a].rearrange("p i (m u e) -> p u m i e", u=2, e=2)
            if scalar_cols > 0:
                nc.scalar.copy(out=dst[:, :, :scalar_cols], in_=src[:, :, :scalar_cols])
            if scalar_cols < P:
                nc.vector.tensor_copy(out=dst[:, :, scalar_cols:], in_=src[:, :, scalar_cols:])
            w1_bf[b, a] = grouped

        def quantise_w1(b, a):
            nc.vector.quantize_mx(out=w1_q[b, a][:].bitcast(FP8X4), scales=w1_sc[b, a][:], in_=w1_bf[b, a][:])

        def gather_v(a, lo, hi):
            nc.vector.tensor_copy(out=v[a][:, lo:hi], in_=tab[a][:].indirect(idx[:, lo // 16 : hi // 16]))

        tanh_sb = {}

        def first_stage(b, lo, hi, tag):
            width = hi - lo
            th = keep.tile([P, PACK, width], F32, name="th", tag=tag)
            per_bank = PASS // width
            for t0 in range(0, PACK, per_bank):
                acc = psum.tile([P, per_bank, width], F32, name="acc1", tag="wide")
                for a in range(2):
                    for u in range(per_bank):
                        ch = slice((t0 + u) * P, (t0 + u + 1) * P)
                        nc.tensor.matmul_mx(
                            out=acc[:, u, :],
                            lhsT=w1_q[b, a][:, ch].bitcast(FP8X4), lhsT_scale=w1_sc[b, a][:, ch],
                            rhs=v[a][:, lo:hi].bitcast(FP8X4), rhs_scale=v_sc[TAB_PLANE + 4 * a :, lo:hi],
                            start=(a == 0 and u == 0), stop=(a == 1 and u == per_bank - 1),
                        )
                nc.scalar.activation(out=th[:, t0 : t0 + per_bank, :], in_=acc[:], func=ACT.Tanh)
            for c in range(lo, hi, P):
                tanh_sb[b, c] = (th, c - lo)

        h_bf, h_q = {}, {}

        def weigh(b, lo, hi):
            hb = ring.tile([P, PACK * (hi - lo)], BF16, name="h_bf", bufs=3, align_bytes=64)
            rel_tile, rel_lo = rel_sb[b, lo]
            th, th_lo = tanh_sb[b, lo]
            nc.vector.tensor_tensor(
                out=hb[:].rearrange("p (c e t) -> p c t e", e=2, t=PACK),
                in0=th[:, :, th_lo : th_lo + hi - lo].rearrange("p t (c e) -> p c t e", e=2),
                in1=rel_tile[:, :, rel_lo : rel_lo + hi - lo].rearrange("p t (c e) -> p c t e", e=2),
                op=ALU.mult,
            )
            h_bf[b, lo] = hb

        def quantise_h(b, lo, hi):
            codes = keep.tile([P, hi - lo], U32, name="h_q%d_%d" % (b, lo), align_bytes=64)
            scales = keep.tile([P, hi - lo], U8, name="h_sc%d_%d" % (b, lo), align_bytes=64)
            nc.vector.quantize_mx(out=codes[:].bitcast(FP8X4), scales=scales[:], in_=h_bf[b, lo][:])
            for c in range(lo, hi, P):
                h_q[b, c] = (codes, scales, c - lo)

        y_banks = {}

        def second_stage(lo, hi):
            half, at = divmod(lo, PASS)
            for n in range(N // P):
                if at == 0:
                    y_banks[n] = psum.tile([P, PASS], F32, name="acc2", tag="second")
                for b in range(2):
                    codes, scales, first = h_q[b, lo]
                    cols = slice(first, first + hi - lo)
                    nc.tensor.matmul_mx(
                        out=y_banks[n][:, at : at + hi - lo],
                        lhsT=w2[:, b, 2 * n * P : 2 * (n + 1) * P].bitcast(FP4X4), lhsT_scale=w2_sc[:, b, n * P : (n + 1) * P],
                        rhs=codes[:, cols].bitcast(FP8X4), rhs_scale=scales[:, cols],
                        start=(b == 0), stop=(b == 1),
                    )
                if hi % PASS == 0:
                    nc.scalar.copy(out=y[n][:, half * PASS : (half + 1) * PASS], in_=y_banks[n][:])

        def expected():
            v2 = keep.tile([P, PICK], U32, name="v2", tag="rel1_512", align_bytes=64)
            nc.vector.tensor_copy(out=v2[:], in_=tab2[:].indirect(idx2[:]))
            banks = []
            for n in range(N // P):
                acc = psum.tile([P, PICK], F32, name="accb", tag="wide")
                nc.tensor.matmul_mx(
                    out=acc[:],
                    lhsT=wp[:, n * P : (n + 1) * P].bitcast(FP8X4), lhsT_scale=wp_sc[:, n * P : (n + 1) * P],
                    rhs=v2[:].bitcast(FP8X4), rhs_scale=v2_sc[TAB2_PLANE:, :],
                    start=True, stop=True,
                )
                banks.append(acc)
            return banks

        for a in range(2):
            round_w1(0, a, P)
            round_w1(1, a, 0)
            quantise_w1(1, a)
            quantise_w1(0, a)
        nc.vector.tensor_copy(out=v_sc[:], in_=tab_sc[:].indirect(idx[:]))
        gather_v(0, 0, S)
        nc.vector.tensor_copy(out=v2_sc[:], in_=tab2_sc[:].indirect(idx2[:]))
        gather_v(1, 0, JC)
        gather_v(1, JC, 2 * JC)
        gather_v(1, 2 * JC, S)
        first_stage(0, 0, 256, "th0")
        first_stage(0, 256, 512, "th1")
        first_stage(1, 0, 512, "w1_raw0")
        first_stage(0, 512, 1024, "w1_raw1")
        first_stage(1, 512, 1024, "th2")

        units = [(0, 0, 256), (0, 256, 512), (1, 0, 512), (0, 512, 1024), (1, 512, 768), (1, 768, 896), (1, 896, 1024)]

        def close(unit):
            quantise_h(*unit)
            if unit[0] == 1:
                for lo in range(unit[1], unit[2], JC):
                    second_stage(lo, min(lo + JC, unit[2]))

        for i, unit in enumerate(units[:-1]):
            weigh(*unit)
            if i > 0:
                close(units[i - 1])
        banks = expected()
        for n in range(2):
            nc.scalar.copy(out=base[n][:], in_=banks[n][:])
        close(units[-2])
        weigh(*units[-1])
        nc.vector.tensor_copy(out=base[2][:], in_=banks[2][:])
        close(units[-1])
        nc.vector.tensor_copy(out=base[3][:], in_=banks[3][:])

        pieces = [(n, 0, PICK) for n in range(N // P - 1)] + [(N // P - 1, 0, PICK // 2), (N // P - 1, PICK // 2, PICK)]
        late = []
        for i, (n, lo, hi) in enumerate(pieces):
            diff = ring.tile([P, hi - lo], F32, name="diff", bufs=3)
            nc.vector.tensor_tensor(out=diff[:], in0=y[n][:].indirect(p1[:, lo // 16 : hi // 16]), in1=base[n][:, lo:hi], op=ALU.subtract)
            size = ring.tile([P, hi - lo], F32, name="size", bufs=3)
            nc.scalar.activation(out=size[:], in_=diff[:], func=ACT.Abs)
            res = ring.tile([P, hi - lo], F32, name="res", bufs=5)
            if i >= len(pieces) - 3:
                late.append((n, lo, hi, size, res))
            else:
                nc.scalar.activation(out=res[:], in_=size[:], func=ACT.Copy, scale=gate_col[:, n : n + 1])
                nc.sync.dma_start(out=out[n * P : (n + 1) * P, lo:hi], in_=res[:])
        for n, lo, hi, size, res in late:
            nc.vector.tensor_scalar(out=res[:], in0=size[:], scalar1=gate_col[:, n : n + 1], scalar2=None, op0=ALU.mult)
            nc.sync.dma_start(out=out[n * P : (n + 1) * P, lo:hi], in_=res[:])
